import numpy as np
import ml_dtypes


def mxq(x, axis, fmt="e4m3"):
    dtype, down = {"e4m3": (ml_dtypes.float8_e4m3fn, 7), "e5m2": (ml_dtypes.float8_e5m2, 14)}[fmt]
    v = np.moveaxis(np.asarray(x, np.float32).astype(ml_dtypes.bfloat16).astype(np.float64), axis, -1)
    blocks = v.reshape(v.shape[:-1] + (-1, 32))
    amax = np.abs(blocks).max(-1, keepdims=True)
    byte = np.maximum(np.where(amax > 0, np.frexp(amax)[1] - 1 + 127, 0) - down, 1)
    scale = np.exp2(byte - 127.0)
    codes = (blocks / scale).astype(np.float32).astype(dtype).astype(np.float64)
    return np.moveaxis((codes * scale).reshape(v.shape), -1, axis)


WIDE = False


def mx_kscale(k):
    if not WIDE:
        return np.ones(k)
    levels = np.array([10, -10, 5, -5, 0])
    if k % 512:
        return np.exp2(np.random.permutation(np.resize(levels, k // 32))).repeat(32)
    a = np.empty((k // 512, 16))
    for p in range(k // 512):
        a[p, :8] = np.random.permutation(np.resize(levels, 8))
        for g in range(8):
            far = levels[np.abs(levels - a[p, g]) >= 10]
            a[p, g + 8] = far[np.random.randint(len(far))]
    return np.exp2(a.ravel()).repeat(32)


def f64(x):
    return np.asarray(x).astype(np.float64)


def striped(idx):
    return np.tile(idx.reshape(-1, 16).T, (8, 1)).astype(np.uint16)


def unstriped(offs):
    return offs[:16].T.reshape(-1).astype(np.int64)


E2M1 = np.array([0.0, 0.5, 1.0, 1.5, 2.0, 3.0, 4.0, 6.0, -0.0, -0.5, -1.0, -1.5, -2.0, -3.0, -4.0, -6.0])


def pack_weight(w, fmt):
    k, n = w.shape
    w = f64(np.asarray(w, np.float32).astype(ml_dtypes.bfloat16)).reshape(k // 32, 32, n)
    amax = np.abs(w).max(1)
    if fmt == "e4m3":
        byte = np.frexp(amax)[1] - 1 + 127 - 7
    else:
        mant, ex = np.frexp(amax / 6.0)
        byte = np.where(mant > 0.5, ex, ex - 1) + 127
    byte = np.clip(np.where(amax > 0, byte, 1), 1, 254)
    scaled = (w * np.exp2(127.0 - byte)[:, None, :]).reshape(k, n).astype(np.float32)
    by_word = np.ascontiguousarray(scaled.reshape(k // 512, 128, 4, n).transpose(0, 1, 3, 2))
    if fmt == "e4m3":
        words = by_word.astype(ml_dtypes.float8_e4m3fn).view(np.uint8)
    else:
        c = by_word.astype(ml_dtypes.float4_e2m1fn).view(np.uint8) & 0xF
        words = (c[..., 0::2] | (c[..., 1::2] << 4)).reshape(k // 512, 128, 2 * n)
    return np.ascontiguousarray(words), np.ascontiguousarray(byte.astype(np.uint8).reshape(k // 512, 16, n))


def unpack_weight(words, scales, fmt):
    g, _, n = scales.shape
    words = np.ascontiguousarray(words).reshape(g, 128, n, -1)
    if fmt == "e4m3":
        vals = words.view(ml_dtypes.float8_e4m3fn).astype(np.float64)
    else:
        nib = np.empty((g, 128, n, 4), np.uint8)
        nib[..., 0::2] = words & 0xF
        nib[..., 1::2] = words >> 4
        vals = E2M1[nib]
    vals = vals * np.repeat(np.exp2(scales.astype(np.float64) - 127.0), 8, axis=1)[..., None]
    return vals.transpose(0, 1, 3, 2).reshape(g * 512, n)


def gelu(v):
    return 0.5 * v * (1.0 + np.tanh(np.sqrt(2.0 / np.pi) * (v + 0.044715 * v**3)))


def bf(x):
    return np.asarray(x, np.float32).astype(ml_dtypes.bfloat16)


def planes(Y):
    n, m = Y.shape
    b = f64(bf(Y)).reshape(n // 32, 32, m)
    amax = np.abs(b).max(1)
    byte = np.clip(np.where(amax > 0, np.frexp(amax)[1] - 1 + 127 - 7, 1), 1, 254)
    codes = (b * np.exp2(127.0 - byte)[:, None, :]).reshape(n, m).astype(np.float32).astype(ml_dtypes.float8_e4m3fn).view(np.uint8)
    words = codes.reshape(n // 512, 128, 4, m).transpose(0, 1, 3, 2)
    return np.ascontiguousarray(words), np.ascontiguousarray(byte.astype(np.uint8).reshape(n // 512, 16, m))


K, T, S, H, T2, P, N = 1536, 2048, 1024, 512, 2048, 1024, 1024


def setup_inputs():
    n = np.random.standard_normal
    s = mx_kscale(K)[:, None]
    u = mx_kscale(H)[:, None]
    tab_words, tab_scales = pack_weight(n((K, T)) * s, "e4m3")
    w1_words, w1_scales = pack_weight(1.5 * n((K, H)) / np.sqrt(K) / s, "e2m1")
    w2 = n((H, N)) / np.sqrt(H) / u * np.exp(0.8 * n(N))
    return {
        "tab_words": tab_words, "tab_scales": tab_scales,
        "offs": striped(np.random.permutation(T)[:S]),
        "w1_words": w1_words, "w1_scales": w1_scales,
        "b1": (0.6 * n(H)).astype(np.float32),
        "gain": (1.3 * np.exp(0.3 * n(H)) * u[:, 0]).astype(np.float32),
        "page0": (0.8 * n((H, T2)) * u).astype(np.float32),
        "wgs": np.exp(0.3 * n((128, S))).astype(np.float32),
        "offs2": striped(np.random.permutation(T2)[:S]),
        "offs3": striped(np.random.permutation(T2)[:P]),
        "offs4": striped(np.random.permutation(T2)[:P]),
        "w2": w2.astype(np.float32),
    }


def reference(tab_words, tab_scales, offs, w1_words, w1_scales, b1, gain,
              page0, wgs, offs2, offs3, offs4, w2):
    v = unpack_weight(tab_words, tab_scales, "e4m3")[:, unstriped(offs)]
    w1 = unpack_weight(w1_words, w1_scales, "e2m1")
    h = np.tanh((w1.T @ v) + f64(b1)[:, None]) * f64(gain)[:, None]
    before = f64(page0)
    page = before.copy()
    page[:, unstriped(offs2)] = np.tile(f64(wgs), (H // 128, 1)) * h
    x = page[:, unstriped(offs3)] - before[:, unstriped(offs4)]
    y = mxq(f64(w2), 0, "e4m3").T @ mxq(x, 0, "e4m3")
    words, scales = planes(y)
    return y, words, scales

@@ -1,0 +1,214 @@
+from contextlib import ExitStack
+
+import concourse.mybir as mybir
+
+K, T, S, H, T2, M, N = 1536, 2048, 1024, 512, 2048, 1024, 1024
+FLOPS = 2 * K * H * S + 2 * H * N * M
+
+F32 = mybir.dt.float32
+BF16 = mybir.dt.bfloat16
+I32 = mybir.dt.int32
+U32 = mybir.dt.uint32
+U16 = mybir.dt.uint16
+U8 = mybir.dt.uint8
+FP8X4 = mybir.dt.float8_e4m3fn_x4
+FP4X4 = mybir.dt.float4_e2m1fn_x4
+MULT = mybir.AluOpType.mult
+SUBTRACT = mybir.AluOpType.subtract
+TANH = mybir.ActivationFunctionType.Tanh
+COPY = mybir.ActivationFunctionType.Copy
+
+P = 128
+PACK = 4
+PASSES = K // (P * PACK)
+GROUPS = N // (P * PACK)
+BANK = 512
+UNIT = 128
+OLD_WIDTH = 256
+CHUNKS = (128, 128, 256, 256, 128, 128)
+
+
+def entries(offsets, first, count):
+    return offsets[:, first // 16 : (first + count) // 16]
+
+
+def tile_list_rivet_growth_features_kernel(
+    tc, tab_words, tab_scales, offs, w1_words, w1_scales, b1, gain, page0, wgs, offs2, offs3, offs4, w2, out_0, out_1, out_2
+):
+    nc = tc.nc
+    with ExitStack() as ctx:
+        keep = ctx.enter_context(tc.tile_pool(name="keep", bufs=1))
+        ring = ctx.enter_context(tc.tile_pool(name="ring", bufs=1))
+        psum = ctx.enter_context(tc.psum_pool(name="psum", bufs=8))
+
+        idx = keep.tile([P, S // 16], U16, name="idx")
+        idx2 = keep.tile([P, S // 16], U16, name="idx2")
+        idx3 = keep.tile([P, M // 16], U16, name="idx3")
+        idx4 = keep.tile([P, M // 16], U16, name="idx4")
+        nc.sync.dma_start(idx[:], offs)
+
+        tab_sc = keep.tile([P, T], U8, name="tab_sc", align_bytes=64)
+        nc.vector.memset(tab_sc[:].bitcast(I32), 0)
+        runs = tab_scales.rearrange("a (h e r) t -> e (a h) r t", e=2, r=4).bitcast(I32)
+        for e in range(2):
+            for first, count in ((0, 4), (4, 2)):
+                rows = slice(32 * e + 4 * first, 32 * e + 4 * (first + count))
+                nc.scalar.dma_start(tab_sc[rows, :].bitcast(I32), runs[e, first : first + count])
+
+        w1_raw = keep.tile([P, PASSES * 2 * H], U8, name="w1_raw", align_bytes=64)
+        nc.sync.dma_start(
+            w1_raw[:].bitcast(I32).rearrange("p (a c) -> p a c", a=PASSES), w1_words.bitcast(I32).rearrange("a p c -> p a c")
+        )
+        tab = [keep.tile([P, T], I32, name=f"tab{a}", align_bytes=64) for a in range(PASSES)]
+        for a in range(PASSES):
+            nc.sync.dma_start(tab[a][:], tab_words[a].rearrange("p t i -> p (t i)").bitcast(I32))
+
+        w1_sc_raw = keep.tile([P, PASSES * H], U8, name="w1_sc_raw", align_bytes=64)
+        nc.gpsimd.memset(w1_sc_raw[:].bitcast(I32), 0)
+        for q in range(4):
+            nc.scalar.dma_start(
+                w1_sc_raw[32 * q : 32 * q + 4, :].bitcast(I32).rearrange("r (a c) -> r a c", a=PASSES),
+                w1_scales.bitcast(I32)[:, 4 * q : 4 * q + 4, :].rearrange("a r c -> r a c"),
+            )
+        bias = keep.tile([P, PACK], F32, name="bias")
+        gains = keep.tile([P, PACK], F32, name="gains")
+        nc.gpsimd.dma_start(bias[:], b1.rearrange("(p t) -> p t", t=PACK))
+        nc.gpsimd.dma_start(gains[:], gain.rearrange("(p t) -> p t", t=PACK))
+
+        nc.sync.dma_start(idx2[:], offs2)
+        page_rows = page0.rearrange("(p t) c -> p t c", t=PACK)
+        page = [keep.tile([P, T2], F32, name=f"page{t}") for t in range(PACK)]
+        wgs_rows = wgs.rearrange("(p t) j -> p t j", t=PACK)
+        wgs_first = keep.tile([P, S], F32, name="wgs_first")
+        wgs_rest = keep.tile([P, PACK - 1, S], F32, name="wgs_rest")
+        nc.sync.dma_start(page[0][:], page_rows[:, 0, :])
+        for q in range(4):
+            nc.sync.dma_start(wgs_first[32 * q : 32 * q + 32, :], wgs_rows[:, 0, :])
+        nc.sync.dma_start(page[1][:], page_rows[:, 1, :])
+        for q in range(4):
+            nc.sync.dma_start(wgs_rest[32 * q : 32 * q + 32, :, :], wgs_rows[:, 1:, :])
+        for t in range(2, PACK):
+            nc.sync.dma_start(page[t][:], page_rows[:, t, :])
+        w2_raw = keep.tile([P, PACK, N], F32, name="w2_raw")
+        nc.sync.dma_start(w2_raw[:], w2.rearrange("(p j) n -> p j n", j=PACK))
+        nc.sync.dma_start(idx3[:], offs3)
+        nc.sync.dma_start(idx4[:], offs4)
+        before = keep.tile([P, PACK, T2], F32, name="before")
+        nc.sync.dma_start(before[:], page_rows)
+
+        picked_sc = keep.tile([P, S], U8, name="picked_sc", align_bytes=64)
+        nc.vector.tensor_copy(picked_sc[:], tab_sc[:].indirect(idx[:]))
+        v_sc = keep.tile([P, PASSES, S], U8, name="v_sc", align_bytes=64)
+        for a in range(PASSES):
+            for h in range(2):
+                first = 4 * (2 * a + h)
+                nc.scalar.dma_start(
+                    v_sc[64 * h : 64 * h + 64, a, :].bitcast(I32), picked_sc[first : first + 64, :].bitcast(I32)
+                )
+
+        w1_codes = keep.tile([P, PASSES * 2 * H], U8, name="w1_codes", align_bytes=64)
+        nc.vector.tensor_copy(
+            w1_codes[:].bitcast(U16).rearrange("p (a t m) -> p a t m", a=PASSES, t=PACK),
+            w1_raw[:].bitcast(U16).rearrange("p (a m t) -> p a t m", a=PASSES, t=PACK),
+        )
+        w1_sc = [keep.tile([P, PASSES, P], U8, name=f"w1_sc{t}", align_bytes=64) for t in range(PACK)]
+        for t in range(PACK):
+            nc.gpsimd.tensor_copy(w1_sc[t][:], w1_sc_raw[:].rearrange("p (a m t) -> p t a m", a=PASSES, t=PACK)[:, t])
+
+        v = [[keep.tile([P, BANK], U32, name=f"v{a}_{h}", align_bytes=64) for h in range(2)] for a in range(PASSES)]
+        for a in range(PASSES):
+            for h in range(2):
+                nc.vector.tensor_copy(v[a][h][:], tab[a][:].bitcast(U32).indirect(entries(idx, h * BANK, BANK)))
+
+        for t in range(PACK):
+            weight = ring.tile([P, S], F32, name="weight", bufs=2)
+            squashed = ring.tile([P, S], F32, name="squashed", bufs=2)
+            rows = wgs_first[:] if t == 0 else wgs_rest[:, t - 1, :]
+            nc.scalar.activation(weight[:], rows, COPY, scale=gains[:, t : t + 1])
+            for h in range(2):
+                cols = slice(h * BANK, (h + 1) * BANK)
+                acc = psum.tile([P, BANK], F32, name="bank")
+                for a in range(PASSES):
+                    first = (a * PACK + t) * P
+                    nc.tensor.matmul_mx(
+                        out=acc[:],
+                        lhsT=w1_codes[:, 2 * first : 2 * (first + P)].bitcast(FP4X4),
+                        lhsT_scale=w1_sc[t][:, a, :],
+                        rhs=v[a][h][:].bitcast(FP8X4),
+                        rhs_scale=v_sc[:, a, cols],
+                        start=(a == 0),
+                        stop=(a == PASSES - 1),
+                    )
+                nc.scalar.activation(squashed[:, cols], acc[:], TANH, bias=bias[:, t : t + 1])
+            width = BANK if t == 0 else S
+            for first in range(0, S, width):
+                cols = slice(first, first + width)
+                nc.vector.tensor_tensor(
+                    page[t][:].indirect(entries(idx2, first, width)), squashed[:, cols], weight[:, cols], MULT
+                )
+
+        w2_bf = keep.tile([P, GROUPS, PACK, P, PACK], BF16, name="w2_bf", align_bytes=64)
+        for g in range(GROUPS):
+            nc.scalar.copy(
+                w2_bf[:, g], w2_raw[:, :, g * BANK : (g + 1) * BANK].rearrange("p j (m t) -> p t m j", t=PACK)
+            )
+        w2_codes = keep.tile([P, N], U32, name="w2_codes", align_bytes=64)
+        w2_sc = keep.tile([P, N], U8, name="w2_sc", align_bytes=64)
+        nc.vector.quantize_mx(
+            out=w2_codes[:].bitcast(FP8X4), scales=w2_sc[:], in_=w2_bf[:].rearrange("p g t m j -> p (g t m j)")
+        )
+
+        y_rows = out_0.rearrange("(g p t) m -> g p t m", g=GROUPS, t=PACK)
+        y_words = out_1.rearrange("g p m t -> p g (m t)").bitcast(I32)
+        y_sc = keep.tile([P, GROUPS, M], U8, name="y_sc", align_bytes=64)
+        nc.gpsimd.memset(y_sc[:].rearrange("p g m -> p (g m)").bitcast(I32), 0)
+        first = 0
+        old = None
+        for width in CHUNKS:
+            cols = slice(first, first + width)
+            if first % OLD_WIDTH == 0:
+                old = ring.tile([P, PACK, OLD_WIDTH], F32, name="old", bufs=1)
+                for t in range(PACK):
+                    nc.vector.tensor_copy(old[:, t, :], before[:, t, :].indirect(entries(idx4, first, OLD_WIDTH)))
+            within = first % OLD_WIDTH
+            x = ring.tile([P, PACK, width], F32, name="x", bufs=1)
+            for t in range(PACK):
+                nc.vector.tensor_tensor(
+                    x[:, t, :], page[t][:].indirect(entries(idx3, first, width)), old[:, t, within : within + width], SUBTRACT
+                )
+            x_bf = ring.tile([P, width, PACK], BF16, name="x_bf", bufs=2, align_bytes=64)
+            nc.scalar.copy(x_bf[:], x[:].rearrange("p t m -> p m t"))
+            x_codes = ring.tile([P, width], U32, name="x_codes", bufs=2, align_bytes=64)
+            x_sc = ring.tile([P, width], U8, name="x_sc", bufs=2, align_bytes=64)
+            nc.vector.quantize_mx(out=x_codes[:].bitcast(FP8X4), scales=x_sc[:], in_=x_bf[:].rearrange("p m t -> p (m t)"))
+
+            y_codes = ring.tile([P, GROUPS, width], I32, name="y_codes", bufs=3, align_bytes=64)
+            for g in range(GROUPS):
+                y = ring.tile([P, PACK, width], F32, name="y", bufs=4)
+                y_bf = ring.tile([P, width, PACK], BF16, name="y_bf", bufs=4, align_bytes=64)
+                for u in range(0, width, UNIT):
+                    unit = slice(u, u + UNIT)
+                    acc = psum.tile([P, PACK, UNIT], F32, name="bank")
+                    for t in range(PACK):
+                        stationary = slice((g * PACK + t) * P, (g * PACK + t + 1) * P)
+                        nc.tensor.matmul_mx(
+                            out=acc[:, t, :],
+                            lhsT=w2_codes[:, stationary].bitcast(FP8X4),
+                            lhsT_scale=w2_sc[:, stationary],
+                            rhs=x_codes[:, unit].bitcast(FP8X4),
+                            rhs_scale=x_sc[:, unit],
+                            start=True,
+                            stop=True,
+                        )
+                    nc.scalar.copy(y_bf[:, unit, :], acc[:].rearrange("p t m -> p m t"))
+                    nc.scalar.copy(y[:, :, unit], acc[:])
+                nc.sync.dma_start(y_rows[g][:, :, cols], y[:])
+                nc.vector.quantize_mx(
+                    out=y_codes[:, g, :].bitcast(FP8X4), scales=y_sc[:, g, cols], in_=y_bf[:].rearrange("p m t -> p (m t)")
+                )
+            nc.sync.dma_start(y_words[:, :, cols], y_codes[:])
+            first += width
+        for q in range(4):
+            nc.sync.dma_start(
+                out_2.bitcast(I32)[:, 4 * q : 4 * q + 4, :].rearrange("g r m -> r g m"), y_sc[32 * q : 32 * q + 4].bitcast(I32)
+            )

@@ -24,8 +24,8 @@ PASSES = K // (P * PACK)
 GROUPS = N // (P * PACK)
 BANK = 512
 UNIT = 128
-OLD_WIDTH = 256
-CHUNKS = (128, 128, 256, 256, 128, 128)
+UNITS = M // UNIT
+SPARE = 8
 
 
 def entries(offsets, first, count):
@@ -47,26 +47,32 @@ def tile_list_rivet_growth_features_kernel(
         idx4 = keep.tile([P, M // 16], U16, name="idx4")
         nc.sync.dma_start(idx[:], offs)
 
-        tab_sc = keep.tile([P, T], U8, name="tab_sc", align_bytes=64)
-        nc.vector.memset(tab_sc[:].bitcast(I32), 0)
+        tab_sc = keep.tile([P, T], U8, name="tab_sc", tag="slot0", align_bytes=64)
+        for rows in (slice(0, SPARE), slice(32, 32 + SPARE), slice(64, P)):
+            nc.vector.memset(tab_sc[rows, :].bitcast(I32), 0)
         runs = tab_scales.rearrange("a (h e r) t -> e (a h) r t", e=2, r=4).bitcast(I32)
         for e in range(2):
             for first, count in ((0, 4), (4, 2)):
-                rows = slice(32 * e + 4 * first, 32 * e + 4 * (first + count))
-                nc.scalar.dma_start(tab_sc[rows, :].bitcast(I32), runs[e, first : first + count])
+                rows = slice(32 * e + SPARE + 4 * first, 32 * e + SPARE + 4 * (first + count))
+                nc.sync.dma_start(tab_sc[rows, :].bitcast(I32), runs[e, first : first + count])
 
-        w1_raw = keep.tile([P, PASSES * 2 * H], U8, name="w1_raw", align_bytes=64)
-        nc.sync.dma_start(
-            w1_raw[:].bitcast(I32).rearrange("p (a c) -> p a c", a=PASSES), w1_words.bitcast(I32).rearrange("a p c -> p a c")
-        )
-        tab = [keep.tile([P, T], I32, name=f"tab{a}", align_bytes=64) for a in range(PASSES)]
+        w1_raw = keep.tile([P, PASSES * 2 * H], U8, name="w1_raw", tag="slot_w1", align_bytes=64)
+        tab = [keep.tile([P, T], I32, name=f"tab{a}", tag=f"slot{a + 1}", align_bytes=64) for a in range(PASSES)]
         for a in range(PASSES):
             nc.sync.dma_start(tab[a][:], tab_words[a].rearrange("p t i -> p (t i)").bitcast(I32))
+            if a == 0:
+                nc.sync.dma_start(
+                    w1_raw[:].bitcast(I32).rearrange("p (a c) -> p a c", a=PASSES),
+                    w1_words.bitcast(I32).rearrange("a p c -> p a c"),
+                )
+                nc.sync.dma_start(idx2[:], offs2)
+                nc.sync.dma_start(idx3[:], offs3)
+                nc.sync.dma_start(idx4[:], offs4)
 
         w1_sc_raw = keep.tile([P, PASSES * H], U8, name="w1_sc_raw", align_bytes=64)
         nc.gpsimd.memset(w1_sc_raw[:].bitcast(I32), 0)
         for q in range(4):
-            nc.scalar.dma_start(
+            nc.gpsimd.dma_start(
                 w1_sc_raw[32 * q : 32 * q + 4, :].bitcast(I32).rearrange("r (a c) -> r a c", a=PASSES),
                 w1_scales.bitcast(I32)[:, 4 * q : 4 * q + 4, :].rearrange("a r c -> r a c"),
             )
@@ -75,38 +81,17 @@ def tile_list_rivet_growth_features_kernel(
         nc.gpsimd.dma_start(bias[:], b1.rearrange("(p t) -> p t", t=PACK))
         nc.gpsimd.dma_start(gains[:], gain.rearrange("(p t) -> p t", t=PACK))
 
-        nc.sync.dma_start(idx2[:], offs2)
-        page_rows = page0.rearrange("(p t) c -> p t c", t=PACK)
-        page = [keep.tile([P, T2], F32, name=f"page{t}") for t in range(PACK)]
-        wgs_rows = wgs.rearrange("(p t) j -> p t j", t=PACK)
-        wgs_first = keep.tile([P, S], F32, name="wgs_first")
-        wgs_rest = keep.tile([P, PACK - 1, S], F32, name="wgs_rest")
-        nc.sync.dma_start(page[0][:], page_rows[:, 0, :])
-        for q in range(4):
-            nc.sync.dma_start(wgs_first[32 * q : 32 * q + 32, :], wgs_rows[:, 0, :])
-        nc.sync.dma_start(page[1][:], page_rows[:, 1, :])
-        for q in range(4):
-            nc.sync.dma_start(wgs_rest[32 * q : 32 * q + 32, :, :], wgs_rows[:, 1:, :])
-        for t in range(2, PACK):
-            nc.sync.dma_start(page[t][:], page_rows[:, t, :])
-        w2_raw = keep.tile([P, PACK, N], F32, name="w2_raw")
-        nc.sync.dma_start(w2_raw[:], w2.rearrange("(p j) n -> p j n", j=PACK))
-        nc.sync.dma_start(idx3[:], offs3)
-        nc.sync.dma_start(idx4[:], offs4)
-        before = keep.tile([P, PACK, T2], F32, name="before")
-        nc.sync.dma_start(before[:], page_rows)
-
-        picked_sc = keep.tile([P, S], U8, name="picked_sc", align_bytes=64)
+        picked_sc = keep.tile([P, S], U8, name="picked_sc", tag="slot_picked", align_bytes=64)
         nc.vector.tensor_copy(picked_sc[:], tab_sc[:].indirect(idx[:]))
         v_sc = keep.tile([P, PASSES, S], U8, name="v_sc", align_bytes=64)
         for a in range(PASSES):
             for h in range(2):
-                first = 4 * (2 * a + h)
-                nc.scalar.dma_start(
+                first = SPARE + 4 * (2 * a + h)
+                nc.sync.dma_start(
                     v_sc[64 * h : 64 * h + 64, a, :].bitcast(I32), picked_sc[first : first + 64, :].bitcast(I32)
                 )
 
-        w1_codes = keep.tile([P, PASSES * 2 * H], U8, name="w1_codes", align_bytes=64)
+        w1_codes = keep.tile([P, PASSES * 2 * H], U8, name="w1_codes", tag="slot_codes", align_bytes=64)
         nc.vector.tensor_copy(
             w1_codes[:].bitcast(U16).rearrange("p (a t m) -> p a t m", a=PASSES, t=PACK),
             w1_raw[:].bitcast(U16).rearrange("p (a m t) -> p a t m", a=PASSES, t=PACK),
@@ -115,19 +100,31 @@ def tile_list_rivet_growth_features_kernel(
         for t in range(PACK):
             nc.gpsimd.tensor_copy(w1_sc[t][:], w1_sc_raw[:].rearrange("p (a m t) -> p t a m", a=PASSES, t=PACK)[:, t])
 
-        v = [[keep.tile([P, BANK], U32, name=f"v{a}_{h}", align_bytes=64) for h in range(2)] for a in range(PASSES)]
+        v = [[keep.tile([P, BANK], U32, name=f"v{a}_{h}", tag=f"slot_v{a}_{h}", align_bytes=64) for h in range(2)] for a in range(PASSES)]
         for a in range(PASSES):
             for h in range(2):
                 nc.vector.tensor_copy(v[a][h][:], tab[a][:].bitcast(U32).indirect(entries(idx, h * BANK, BANK)))
 
+        page_rows = page0.rearrange("(p t) c -> p t c", t=PACK)
+        page = [keep.tile([P, T2], F32, name=f"page{t}", tag=f"slot{t}", align_bytes=64) for t in range(PACK)]
+        wgs_rows = wgs.rearrange("(p t) j -> p t j", t=PACK)
+        wgs_first = keep.tile([P, S], F32, name="wgs_first", tag="slot_w1", align_bytes=64)
+        wgs_rest = keep.tile([P, PACK - 1, S], F32, name="wgs_rest", tag="slot_picked", align_bytes=64)
+        nc.sync.dma_start(page[0][:], page_rows[:, 0, :])
+        for q in range(4):
+            nc.sync.dma_start(wgs_first[32 * q : 32 * q + 32, :], wgs_rows[:, 0, :])
+        nc.sync.dma_start(page[1][:], page_rows[:, 1, :])
+        for q in range(4):
+            nc.sync.dma_start(wgs_rest[32 * q : 32 * q + 32, :, :], wgs_rows[:, 1:, :])
+        for t in range(2, PACK):
+            nc.sync.dma_start(page[t][:], page_rows[:, t, :])
+
         for t in range(PACK):
-            weight = ring.tile([P, S], F32, name="weight", bufs=2)
-            squashed = ring.tile([P, S], F32, name="squashed", bufs=2)
-            rows = wgs_first[:] if t == 0 else wgs_rest[:, t - 1, :]
-            nc.scalar.activation(weight[:], rows, COPY, scale=gains[:, t : t + 1])
+            squashed = keep.tile([P, S], F32, name=f"squashed{t}")
+            weight = wgs_first[:] if t == 0 else wgs_rest[:, t - 1, :]
             for h in range(2):
                 cols = slice(h * BANK, (h + 1) * BANK)
-                acc = psum.tile([P, BANK], F32, name="bank")
+                acc = psum.tile([P, BANK], F32, name="h_bank", bufs=2)
                 for a in range(PASSES):
                     first = (a * PACK + t) * P
                     nc.tensor.matmul_mx(
@@ -140,6 +137,7 @@ def tile_list_rivet_growth_features_kernel(
                         stop=(a == PASSES - 1),
                     )
                 nc.scalar.activation(squashed[:, cols], acc[:], TANH, bias=bias[:, t : t + 1])
+                nc.scalar.activation(squashed[:, cols], squashed[:, cols], COPY, scale=gains[:, t : t + 1])
             width = BANK if t == 0 else S
             for first in range(0, S, width):
                 cols = slice(first, first + width)
@@ -147,6 +145,10 @@ def tile_list_rivet_growth_features_kernel(
                     page[t][:].indirect(entries(idx2, first, width)), squashed[:, cols], weight[:, cols], MULT
                 )
 
+        w2_raw = keep.tile([P, PACK, N], F32, name="w2_raw", tag="slot_v0_0", align_bytes=64)
+        nc.sync.dma_start(w2_raw[:], w2.rearrange("(p j) n -> p j n", j=PACK))
+        before = keep.tile([P, PACK, T2], F32, name="before", tag="slot_codes", align_bytes=64)
+        nc.sync.dma_start(before[:], page_rows)
         w2_bf = keep.tile([P, GROUPS, PACK, P, PACK], BF16, name="w2_bf", align_bytes=64)
         for g in range(GROUPS):
             nc.scalar.copy(
@@ -161,53 +163,71 @@ def tile_list_rivet_growth_features_kernel(
         y_rows = out_0.rearrange("(g p t) m -> g p t m", g=GROUPS, t=PACK)
         y_words = out_1.rearrange("g p m t -> p g (m t)").bitcast(I32)
         y_sc = keep.tile([P, GROUPS, M], U8, name="y_sc", align_bytes=64)
-        nc.gpsimd.memset(y_sc[:].rearrange("p g m -> p (g m)").bitcast(I32), 0)
-        first = 0
-        old = None
-        for width in CHUNKS:
-            cols = slice(first, first + width)
-            if first % OLD_WIDTH == 0:
-                old = ring.tile([P, PACK, OLD_WIDTH], F32, name="old", bufs=1)
-                for t in range(PACK):
-                    nc.vector.tensor_copy(old[:, t, :], before[:, t, :].indirect(entries(idx4, first, OLD_WIDTH)))
-            within = first % OLD_WIDTH
-            x = ring.tile([P, PACK, width], F32, name="x", bufs=1)
+        old = {}
+        banks = {}
+
+        def fetch_old(pair, half, tag):
+            tile = ring.tile([P, 2, 2 * UNIT], F32, name="old", tag=tag, bufs=1, align_bytes=64)
+            for e in range(2):
+                t = 2 * half + e
+                nc.vector.tensor_copy(tile[:, e, :], before[:, t, :].indirect(entries(idx4, 2 * UNIT * pair, 2 * UNIT)))
+                old[pair, t] = tile[:, e, :]
+
+        def multiply(c):
+            x = ring.tile([P, PACK, UNIT], F32, name="x", bufs=2)
+            within = slice((c % 2) * UNIT, (c % 2 + 1) * UNIT)
             for t in range(PACK):
                 nc.vector.tensor_tensor(
-                    x[:, t, :], page[t][:].indirect(entries(idx3, first, width)), old[:, t, within : within + width], SUBTRACT
+                    x[:, t, :], page[t][:].indirect(entries(idx3, c * UNIT, UNIT)), old[c // 2, t][:, within], SUBTRACT
                 )
-            x_bf = ring.tile([P, width, PACK], BF16, name="x_bf", bufs=2, align_bytes=64)
-            nc.scalar.copy(x_bf[:], x[:].rearrange("p t m -> p m t"))
-            x_codes = ring.tile([P, width], U32, name="x_codes", bufs=2, align_bytes=64)
-            x_sc = ring.tile([P, width], U8, name="x_sc", bufs=2, align_bytes=64)
+            x_bf = ring.tile([P, UNIT, PACK], BF16, name="x_bf", tag=f"stage{c}", bufs=1, align_bytes=64)
+            if c == UNITS - 1:
+                nc.vector.tensor_copy(x_bf[:], x[:].rearrange("p t m -> p m t"))
+            else:
+                nc.scalar.copy(x_bf[:], x[:].rearrange("p t m -> p m t"))
+            x_codes = ring.tile([P, UNIT], U32, name="x_codes", bufs=2, align_bytes=64)
+            x_sc = ring.tile([P, UNIT], U8, name="x_sc", bufs=2, align_bytes=64)
             nc.vector.quantize_mx(out=x_codes[:].bitcast(FP8X4), scales=x_sc[:], in_=x_bf[:].rearrange("p m t -> p (m t)"))
-
-            y_codes = ring.tile([P, GROUPS, width], I32, name="y_codes", bufs=3, align_bytes=64)
             for g in range(GROUPS):
-                y = ring.tile([P, PACK, width], F32, name="y", bufs=4)
-                y_bf = ring.tile([P, width, PACK], BF16, name="y_bf", bufs=4, align_bytes=64)
-                for u in range(0, width, UNIT):
-                    unit = slice(u, u + UNIT)
-                    acc = psum.tile([P, PACK, UNIT], F32, name="bank")
-                    for t in range(PACK):
-                        stationary = slice((g * PACK + t) * P, (g * PACK + t + 1) * P)
-                        nc.tensor.matmul_mx(
-                            out=acc[:, t, :],
-                            lhsT=w2_codes[:, stationary].bitcast(FP8X4),
-                            lhsT_scale=w2_sc[:, stationary],
-                            rhs=x_codes[:, unit].bitcast(FP8X4),
-                            rhs_scale=x_sc[:, unit],
-                            start=True,
-                            stop=True,
-                        )
-                    nc.scalar.copy(y_bf[:, unit, :], acc[:].rearrange("p t m -> p m t"))
-                    nc.scalar.copy(y[:, :, unit], acc[:])
+                acc = psum.tile([P, PACK, UNIT], F32, name="y_bank", bufs=6)
+                for t in range(PACK):
+                    stationary = slice((g * PACK + t) * P, (g * PACK + t + 1) * P)
+                    nc.tensor.matmul_mx(
+                        out=acc[:, t, :],
+                        lhsT=w2_codes[:, stationary].bitcast(FP8X4),
+                        lhsT_scale=w2_sc[:, stationary],
+                        rhs=x_codes[:].bitcast(FP8X4),
+                        rhs_scale=x_sc[:],
+                        start=True,
+                        stop=True,
+                    )
+                banks[c, g] = acc
+
+        def hand_out(c):
+            cols = slice(c * UNIT, (c + 1) * UNIT)
+            y_codes = ring.tile([P, GROUPS, UNIT], I32, name="y_codes", bufs=4, align_bytes=64)
+            for g in range(GROUPS):
+                copy = nc.vector.tensor_copy if (c, g) == (UNITS - 1, GROUPS - 1) else nc.scalar.copy
+                y = ring.tile([P, PACK, UNIT], F32, name="y", bufs=6)
+                y_bf = ring.tile([P, UNIT, PACK], BF16, name="y_bf", bufs=4, align_bytes=64)
+                copy(y_bf[:], banks[c, g][:].rearrange("p t m -> p m t"))
+                copy(y[:], banks[c, g][:])
                 nc.sync.dma_start(y_rows[g][:, :, cols], y[:])
                 nc.vector.quantize_mx(
                     out=y_codes[:, g, :].bitcast(FP8X4), scales=y_sc[:, g, cols], in_=y_bf[:].rearrange("p m t -> p (m t)")
                 )
             nc.sync.dma_start(y_words[:, :, cols], y_codes[:])
-            first += width
+
+        for half in range(2):
+            fetch_old(0, half, f"first_old{half}")
+        for pair in range(UNITS // 2):
+            for half in range(2):
+                multiply(2 * pair + half)
+            if pair + 1 < UNITS // 2:
+                for half in range(2):
+                    fetch_old(pair + 1, half, f"stage{2 * pair + half}")
+            for half in range(2):
+                hand_out(2 * pair + half)
         for q in range(4):
             nc.sync.dma_start(
                 out_2.bitcast(I32)[:, 4 * q : 4 * q + 4, :].rearrange("g r m -> r g m"), y_sc[32 * q : 32 * q + 4].bitcast(I32)

@@ -1,6 +1,7 @@
 from contextlib import ExitStack
 
 import concourse.mybir as mybir
+from concourse.masks import make_identity
 
 K, T, S, H, T2, M, N = 1536, 2048, 1024, 512, 2048, 1024, 1024
 FLOPS = 2 * K * H * S + 2 * H * N * M
@@ -24,7 +25,7 @@ PASSES = K // (P * PACK)
 GROUPS = N // (P * PACK)
 BANK = 512
 UNIT = 128
-UNITS = M // UNIT
+WIDTHS = (128, 256, 256, 256, 128)
 SPARE = 8
 
 
@@ -56,30 +57,25 @@ def tile_list_rivet_growth_features_kernel(
                 rows = slice(32 * e + SPARE + 4 * first, 32 * e + SPARE + 4 * (first + count))
                 nc.sync.dma_start(tab_sc[rows, :].bitcast(I32), runs[e, first : first + count])
 
-        w1_raw = keep.tile([P, PASSES * 2 * H], U8, name="w1_raw", tag="slot_w1", align_bytes=64)
         tab = [keep.tile([P, T], I32, name=f"tab{a}", tag=f"slot{a + 1}", align_bytes=64) for a in range(PASSES)]
-        for a in range(PASSES):
-            nc.sync.dma_start(tab[a][:], tab_words[a].rearrange("p t i -> p (t i)").bitcast(I32))
-            if a == 0:
-                nc.sync.dma_start(
-                    w1_raw[:].bitcast(I32).rearrange("p (a c) -> p a c", a=PASSES),
-                    w1_words.bitcast(I32).rearrange("a p c -> p a c"),
-                )
-                nc.sync.dma_start(idx2[:], offs2)
-                nc.sync.dma_start(idx3[:], offs3)
-                nc.sync.dma_start(idx4[:], offs4)
-
+        tab_rows = tab_words.rearrange("a p t i -> a p (t i)").bitcast(I32)
+        nc.sync.dma_start(tab[0][:], tab_rows[0])
+        w1_raw = keep.tile([P, PASSES * 2 * H], U8, name="w1_raw", align_bytes=64)
+        nc.sync.dma_start(
+            w1_raw[:].bitcast(I32).rearrange("p (a c) -> p a c", a=PASSES), w1_words.bitcast(I32).rearrange("a p c -> p a c")
+        )
+        nc.sync.dma_start(tab[1][:], tab_rows[1])
         w1_sc_raw = keep.tile([P, PASSES * H], U8, name="w1_sc_raw", align_bytes=64)
         nc.gpsimd.memset(w1_sc_raw[:].bitcast(I32), 0)
         for q in range(4):
-            nc.gpsimd.dma_start(
+            nc.sync.dma_start(
                 w1_sc_raw[32 * q : 32 * q + 4, :].bitcast(I32).rearrange("r (a c) -> r a c", a=PASSES),
                 w1_scales.bitcast(I32)[:, 4 * q : 4 * q + 4, :].rearrange("a r c -> r a c"),
             )
-        bias = keep.tile([P, PACK], F32, name="bias")
-        gains = keep.tile([P, PACK], F32, name="gains")
-        nc.gpsimd.dma_start(bias[:], b1.rearrange("(p t) -> p t", t=PACK))
-        nc.gpsimd.dma_start(gains[:], gain.rearrange("(p t) -> p t", t=PACK))
+        wgs_raw = keep.tile([P, S], F32, name="wgs_raw", align_bytes=64)
+        nc.sync.dma_start(wgs_raw[:], wgs)
+        identity = keep.tile([P, P], F32, name="identity")
+        make_identity(nc, identity[:])
 
         picked_sc = keep.tile([P, S], U8, name="picked_sc", tag="slot_picked", align_bytes=64)
         nc.vector.tensor_copy(picked_sc[:], tab_sc[:].indirect(idx[:]))
@@ -91,14 +87,23 @@ def tile_list_rivet_growth_features_kernel(
                     v_sc[64 * h : 64 * h + 64, a, :].bitcast(I32), picked_sc[first : first + 64, :].bitcast(I32)
                 )
 
+        nc.sync.dma_start(tab[2][:], tab_rows[2])
+        nc.sync.dma_start(idx2[:], offs2)
+        row_constants = keep.tile([P, 2, 8], F32, name="row_constants", align_bytes=64)
+        bias, gains = row_constants[:, 0, :], row_constants[:, 1, :]
+        nc.sync.dma_start(bias[:, :PACK], b1.rearrange("(p t) -> p t", t=PACK))
+        nc.sync.dma_start(gains[:, :PACK], gain.rearrange("(p t) -> p t", t=PACK))
+
         w1_codes = keep.tile([P, PASSES * 2 * H], U8, name="w1_codes", tag="slot_codes", align_bytes=64)
         nc.vector.tensor_copy(
-            w1_codes[:].bitcast(U16).rearrange("p (a t m) -> p a t m", a=PASSES, t=PACK),
-            w1_raw[:].bitcast(U16).rearrange("p (a m t) -> p a t m", a=PASSES, t=PACK),
+            w1_codes[:].bitcast(U16).rearrange("p (a t c i) -> p a c t i", a=PASSES, t=PACK, i=8),
+            w1_raw[:].bitcast(U16).rearrange("p (a c i t) -> p a c t i", a=PASSES, t=PACK, i=8),
         )
-        w1_sc = [keep.tile([P, PASSES, P], U8, name=f"w1_sc{t}", align_bytes=64) for t in range(PACK)]
-        for t in range(PACK):
-            nc.gpsimd.tensor_copy(w1_sc[t][:], w1_sc_raw[:].rearrange("p (a m t) -> p t a m", a=PASSES, t=PACK)[:, t])
+        w1_sc = keep.tile([P, PASSES * H], U8, name="w1_sc", align_bytes=64)
+        nc.vector.tensor_copy(
+            w1_sc[:].rearrange("p (a t c i) -> p a c t i", a=PASSES, t=PACK, i=16),
+            w1_sc_raw[:].rearrange("p (a c i t) -> p a c t i", a=PASSES, t=PACK, i=16),
+        )
 
         v = [[keep.tile([P, BANK], U32, name=f"v{a}_{h}", tag=f"slot_v{a}_{h}", align_bytes=64) for h in range(2)] for a in range(PASSES)]
         for a in range(PASSES):
@@ -107,21 +112,35 @@ def tile_list_rivet_growth_features_kernel(
 
         page_rows = page0.rearrange("(p t) c -> p t c", t=PACK)
         page = [keep.tile([P, T2], F32, name=f"page{t}", tag=f"slot{t}", align_bytes=64) for t in range(PACK)]
-        wgs_rows = wgs.rearrange("(p t) j -> p t j", t=PACK)
-        wgs_first = keep.tile([P, S], F32, name="wgs_first", tag="slot_w1", align_bytes=64)
-        wgs_rest = keep.tile([P, PACK - 1, S], F32, name="wgs_rest", tag="slot_picked", align_bytes=64)
+        nc.sync.dma_start(idx4[:], offs4)
         nc.sync.dma_start(page[0][:], page_rows[:, 0, :])
-        for q in range(4):
-            nc.sync.dma_start(wgs_first[32 * q : 32 * q + 32, :], wgs_rows[:, 0, :])
-        nc.sync.dma_start(page[1][:], page_rows[:, 1, :])
-        for q in range(4):
-            nc.sync.dma_start(wgs_rest[32 * q : 32 * q + 32, :, :], wgs_rows[:, 1:, :])
-        for t in range(2, PACK):
+        nc.sync.dma_start(idx3[:], offs3)
+        old_first = keep.tile([P, M], F32, name="old_first", align_bytes=64)
+        nc.vector.tensor_copy(old_first[:], page[0][:].indirect(idx4[:]))
+        for t in range(1, PACK):
             nc.sync.dma_start(page[t][:], page_rows[:, t, :])
+
+        turned = []
+        for h in range(2):
+            bank = psum.tile([P, PACK, P], F32, name="y_bank", bufs=6)
+            for i in range(PACK):
+                first = h * BANK + i * P
+                nc.tensor.transpose(bank[:, i, :], wgs_raw[:, first : first + P], identity[:])
+            turned.append(bank)
 
         for t in range(PACK):
             squashed = keep.tile([P, S], F32, name=f"squashed{t}")
-            weight = wgs_first[:] if t == 0 else wgs_rest[:, t - 1, :]
+            weight = keep.tile([P, S], F32, name=f"weight{t}", tag=f"slot_weight{t}", align_bytes=64)
+            for h in range(2):
+                dealt = ring.tile([P, PACK, 4, 32], F32, name="dealt", bufs=2)
+                rows = turned[h][:].rearrange("j i (u t) -> j t i u", t=PACK)[:, t]
+                nc.scalar.copy(dealt[:], rows.unsqueeze(2).to_broadcast([P, PACK, 4, 32]))
+                bank = psum.tile([P, PACK, P], F32, name="y_bank", bufs=6)
+                for i in range(PACK):
+                    nc.tensor.transpose(bank[:, i, :], dealt[:, i].rearrange("j q u -> j (q u)"), identity[:])
+                nc.scalar.activation(
+                    weight[:, h * BANK : (h + 1) * BANK], bank[:].rearrange("p i j -> p (i j)"), COPY, scale=gains[:, t : t + 1]
+                )
             for h in range(2):
                 cols = slice(h * BANK, (h + 1) * BANK)
                 acc = psum.tile([P, BANK], F32, name="h_bank", bufs=2)
@@ -130,14 +149,13 @@ def tile_list_rivet_growth_features_kernel(
                     nc.tensor.matmul_mx(
                         out=acc[:],
                         lhsT=w1_codes[:, 2 * first : 2 * (first + P)].bitcast(FP4X4),
-                        lhsT_scale=w1_sc[t][:, a, :],
+                        lhsT_scale=w1_sc[:, first : first + P],
                         rhs=v[a][h][:].bitcast(FP8X4),
                         rhs_scale=v_sc[:, a, cols],
                         start=(a == 0),
                         stop=(a == PASSES - 1),
                     )
                 nc.scalar.activation(squashed[:, cols], acc[:], TANH, bias=bias[:, t : t + 1])
-                nc.scalar.activation(squashed[:, cols], squashed[:, cols], COPY, scale=gains[:, t : t + 1])
             width = BANK if t == 0 else S
             for first in range(0, S, width):
                 cols = slice(first, first + width)
@@ -147,14 +165,17 @@ def tile_list_rivet_growth_features_kernel(
 
         w2_raw = keep.tile([P, PACK, N], F32, name="w2_raw", tag="slot_v0_0", align_bytes=64)
         nc.sync.dma_start(w2_raw[:], w2.rearrange("(p j) n -> p j n", j=PACK))
-        before = keep.tile([P, PACK, T2], F32, name="before", tag="slot_codes", align_bytes=64)
-        nc.sync.dma_start(before[:], page_rows)
+        before = {}
+        for t in range(1, PACK):
+            before[t] = keep.tile([P, T2], F32, name=f"before{t}", tag=f"slot_v{t - 1}_1", align_bytes=64)
+            nc.sync.dma_start(before[t][:], page_rows[:, t, :])
         w2_bf = keep.tile([P, GROUPS, PACK, P, PACK], BF16, name="w2_bf", align_bytes=64)
         for g in range(GROUPS):
             nc.scalar.copy(
-                w2_bf[:, g], w2_raw[:, :, g * BANK : (g + 1) * BANK].rearrange("p j (m t) -> p t m j", t=PACK)
+                w2_bf[:, g].rearrange("p t m j -> p m t j"),
+                w2_raw[:, :, g * BANK : (g + 1) * BANK].rearrange("p j (m t) -> p m t j", t=PACK),
             )
-        w2_codes = keep.tile([P, N], U32, name="w2_codes", align_bytes=64)
+        w2_codes = keep.tile([P, N], U32, name="w2_codes", tag=f"slot_weight{PACK - 1}", align_bytes=64)
         w2_sc = keep.tile([P, N], U8, name="w2_sc", align_bytes=64)
         nc.vector.quantize_mx(
             out=w2_codes[:].bitcast(FP8X4), scales=w2_sc[:], in_=w2_bf[:].rearrange("p g t m j -> p (g t m j)")
@@ -163,71 +184,72 @@ def tile_list_rivet_growth_features_kernel(
         y_rows = out_0.rearrange("(g p t) m -> g p t m", g=GROUPS, t=PACK)
         y_words = out_1.rearrange("g p m t -> p g (m t)").bitcast(I32)
         y_sc = keep.tile([P, GROUPS, M], U8, name="y_sc", align_bytes=64)
+        starts = [sum(WIDTHS[:k]) for k in range(len(WIDTHS))]
+        last = len(WIDTHS) - 1
         old = {}
         banks = {}
+        codes = {}
 
-        def fetch_old(pair, half, tag):
-            tile = ring.tile([P, 2, 2 * UNIT], F32, name="old", tag=tag, bufs=1, align_bytes=64)
-            for e in range(2):
-                t = 2 * half + e
-                nc.vector.tensor_copy(tile[:, e, :], before[:, t, :].indirect(entries(idx4, 2 * UNIT * pair, 2 * UNIT)))
-                old[pair, t] = tile[:, e, :]
+        def fetch_old(k):
+            for t in range(1, PACK):
+                old[k, t] = ring.tile([P, WIDTHS[k]], F32, name=f"old{t}", bufs=1, align_bytes=64)
+                nc.vector.tensor_copy(old[k, t][:], before[t][:].indirect(entries(idx4, starts[k], WIDTHS[k])))
 
-        def multiply(c):
-            x = ring.tile([P, PACK, UNIT], F32, name="x", bufs=2)
-            within = slice((c % 2) * UNIT, (c % 2 + 1) * UNIT)
+        def multiply(k):
+            width = WIDTHS[k]
+            x = ring.tile([P, PACK, width], F32, name="x", bufs=1)
             for t in range(PACK):
-                nc.vector.tensor_tensor(
-                    x[:, t, :], page[t][:].indirect(entries(idx3, c * UNIT, UNIT)), old[c // 2, t][:, within], SUBTRACT
-                )
-            x_bf = ring.tile([P, UNIT, PACK], BF16, name="x_bf", tag=f"stage{c}", bufs=1, align_bytes=64)
-            if c == UNITS - 1:
-                nc.vector.tensor_copy(x_bf[:], x[:].rearrange("p t m -> p m t"))
-            else:
-                nc.scalar.copy(x_bf[:], x[:].rearrange("p t m -> p m t"))
-            x_codes = ring.tile([P, UNIT], U32, name="x_codes", bufs=2, align_bytes=64)
-            x_sc = ring.tile([P, UNIT], U8, name="x_sc", bufs=2, align_bytes=64)
+                reference = old_first[:, starts[k] : starts[k] + width] if t == 0 else old[k, t][:]
+                nc.vector.tensor_tensor(x[:, t, :], page[t][:].indirect(entries(idx3, starts[k], width)), reference, SUBTRACT)
+            x_bf = ring.tile([P, width, PACK], BF16, name="x_bf", bufs=2, align_bytes=64)
+            copy = nc.vector.tensor_copy if k == last else nc.scalar.copy
+            copy(x_bf[:].rearrange("p (c i) t -> p c t i", i=4), x[:].rearrange("p t (c i) -> p c t i", i=4))
+            x_codes = ring.tile([P, width], U32, name="x_codes", bufs=2, align_bytes=64)
+            x_sc = ring.tile([P, width], U8, name="x_sc", bufs=2, align_bytes=64)
             nc.vector.quantize_mx(out=x_codes[:].bitcast(FP8X4), scales=x_sc[:], in_=x_bf[:].rearrange("p m t -> p (m t)"))
             for g in range(GROUPS):
-                acc = psum.tile([P, PACK, UNIT], F32, name="y_bank", bufs=6)
-                for t in range(PACK):
-                    stationary = slice((g * PACK + t) * P, (g * PACK + t + 1) * P)
-                    nc.tensor.matmul_mx(
-                        out=acc[:, t, :],
-                        lhsT=w2_codes[:, stationary].bitcast(FP8X4),
-                        lhsT_scale=w2_sc[:, stationary],
-                        rhs=x_codes[:].bitcast(FP8X4),
-                        rhs_scale=x_sc[:],
-                        start=True,
-                        stop=True,
-                    )
-                banks[c, g] = acc
+                for first in range(0, width, UNIT):
+                    acc = psum.tile([P, PACK, UNIT], F32, name="y_bank", bufs=6)
+                    for t in range(PACK):
+                        stationary = slice((g * PACK + t) * P, (g * PACK + t + 1) * P)
+                        nc.tensor.matmul_mx(
+                            out=acc[:, t, :],
+                            lhsT=w2_codes[:, stationary].bitcast(FP8X4),
+                            lhsT_scale=w2_sc[:, stationary],
+                            rhs=x_codes[:, first : first + UNIT].bitcast(FP8X4),
+                            rhs_scale=x_sc[:, first : first + UNIT],
+                            start=True,
+                            stop=True,
+                        )
+                    banks[k, g, first] = acc
 
-        def hand_out(c):
-            cols = slice(c * UNIT, (c + 1) * UNIT)
-            y_codes = ring.tile([P, GROUPS, UNIT], I32, name="y_codes", bufs=4, align_bytes=64)
-            for g in range(GROUPS):
-                copy = nc.vector.tensor_copy if (c, g) == (UNITS - 1, GROUPS - 1) else nc.scalar.copy
-                y = ring.tile([P, PACK, UNIT], F32, name="y", bufs=6)
-                y_bf = ring.tile([P, UNIT, PACK], BF16, name="y_bf", bufs=4, align_bytes=64)
-                copy(y_bf[:], banks[c, g][:].rearrange("p t m -> p m t"))
-                copy(y[:], banks[c, g][:])
-                nc.sync.dma_start(y_rows[g][:, :, cols], y[:])
-                nc.vector.quantize_mx(
-                    out=y_codes[:, g, :].bitcast(FP8X4), scales=y_sc[:, g, cols], in_=y_bf[:].rearrange("p m t -> p (m t)")
-                )
-            nc.sync.dma_start(y_words[:, :, cols], y_codes[:])
+        def hand_out(k, g):
+            width = WIDTHS[k]
+            cols = slice(starts[k], starts[k] + width)
+            if g == 0:
+                codes[k] = ring.tile([P, GROUPS, width], I32, name="y_codes", bufs=3, align_bytes=64)
+            copy = nc.vector.tensor_copy if (k, g) == (last, GROUPS - 1) else nc.scalar.copy
+            y = ring.tile([P, PACK, width], F32, name="y", bufs=4)
+            y_bf = ring.tile([P, width, PACK], BF16, name="y_bf", bufs=4, align_bytes=64)
+            for first in range(0, width, UNIT):
+                copy(y_bf[:, first : first + UNIT, :], banks[k, g, first][:].rearrange("p t m -> p m t"))
+                copy(y[:, :, first : first + UNIT], banks[k, g, first][:])
+            nc.sync.dma_start(y_rows[g][:, :, cols], y[:])
+            nc.vector.quantize_mx(
+                out=codes[k][:, g, :].bitcast(FP8X4), scales=y_sc[:, g, cols], in_=y_bf[:].rearrange("p m t -> p (m t)")
+            )
+            if g == GROUPS - 1:
+                nc.sync.dma_start(y_words[:, :, cols], codes[k][:])
 
-        for half in range(2):
-            fetch_old(0, half, f"first_old{half}")
-        for pair in range(UNITS // 2):
-            for half in range(2):
-                multiply(2 * pair + half)
-            if pair + 1 < UNITS // 2:
-                for half in range(2):
-                    fetch_old(pair + 1, half, f"stage{2 * pair + half}")
-            for half in range(2):
-                hand_out(2 * pair + half)
+        fetch_old(0)
+        for k in range(len(WIDTHS)):
+            multiply(k)
+            if k < last:
+                fetch_old(k + 1)
+            if k > 0:
+                hand_out(k - 1, 1)
+            hand_out(k, 0)
+        hand_out(last, 1)
         for q in range(4):
             nc.sync.dma_start(
                 out_2.bitcast(I32)[:, 4 * q : 4 * q + 4, :].rearrange("g r m -> r g m"), y_sc[32 * q : 32 * q + 4].bitcast(I32)

@@ -25,8 +25,11 @@ PASSES = K // (P * PACK)
 GROUPS = N // (P * PACK)
 BANK = 512
 UNIT = 128
-WIDTHS = (128, 256, 256, 256, 128)
+WIDTHS = (256, 256, 256, 256)
 SPARE = 8
+RUN = 4
+EARLY = 2
+SHARED_FROM = 2
 
 
 def entries(offsets, first, count):
@@ -46,6 +49,10 @@ def tile_list_rivet_growth_features_kernel(
         idx2 = keep.tile([P, S // 16], U16, name="idx2")
         idx3 = keep.tile([P, M // 16], U16, name="idx3")
         idx4 = keep.tile([P, M // 16], U16, name="idx4")
+        w1_raw = keep.tile([P, PASSES * 2 * H], U8, name="w1_raw", align_bytes=64)
+        nc.sync.dma_start(
+            w1_raw[:].bitcast(I32).rearrange("p (a c) -> p a c", a=PASSES), w1_words.bitcast(I32).rearrange("a p c -> p a c")
+        )
         nc.sync.dma_start(idx[:], offs)
 
         tab_sc = keep.tile([P, T], U8, name="tab_sc", tag="slot0", align_bytes=64)
@@ -59,12 +66,16 @@ def tile_list_rivet_growth_features_kernel(
 
         tab = [keep.tile([P, T], I32, name=f"tab{a}", tag=f"slot{a + 1}", align_bytes=64) for a in range(PASSES)]
         tab_rows = tab_words.rearrange("a p t i -> a p (t i)").bitcast(I32)
-        nc.sync.dma_start(tab[0][:], tab_rows[0])
-        w1_raw = keep.tile([P, PASSES * 2 * H], U8, name="w1_raw", align_bytes=64)
-        nc.sync.dma_start(
-            w1_raw[:].bitcast(I32).rearrange("p (a c) -> p a c", a=PASSES), w1_words.bitcast(I32).rearrange("a p c -> p a c")
-        )
-        nc.sync.dma_start(tab[1][:], tab_rows[1])
+        for a in range(PASSES - 1):
+            nc.sync.dma_start(tab[a][:], tab_rows[a])
+        constant_rows = keep.tile([P, H], F32, name="constant_rows", align_bytes=64)
+        for rows in (slice(0, 30), slice(32, 64), slice(64, P)):
+            nc.gpsimd.memset(constant_rows[rows, :], 0.0)
+        nc.sync.dma_start(constant_rows[30:31, :], b1.rearrange("(o r) -> o r", o=1))
+        nc.sync.dma_start(constant_rows[31:32, :], gain.rearrange("(o r) -> o r", o=1))
+        nc.sync.dma_start(tab[PASSES - 1][:], tab_rows[PASSES - 1])
+        wgs_raw = [keep.tile([P, BANK], F32, name="wgs_raw0", align_bytes=64)]
+        nc.sync.dma_start(wgs_raw[0][:], wgs[:, :BANK])
         w1_sc_raw = keep.tile([P, PASSES * H], U8, name="w1_sc_raw", align_bytes=64)
         nc.gpsimd.memset(w1_sc_raw[:].bitcast(I32), 0)
         for q in range(4):
@@ -72,37 +83,37 @@ def tile_list_rivet_growth_features_kernel(
                 w1_sc_raw[32 * q : 32 * q + 4, :].bitcast(I32).rearrange("r (a c) -> r a c", a=PASSES),
                 w1_scales.bitcast(I32)[:, 4 * q : 4 * q + 4, :].rearrange("a r c -> r a c"),
             )
-        wgs_raw = keep.tile([P, S], F32, name="wgs_raw", align_bytes=64)
-        nc.sync.dma_start(wgs_raw[:], wgs)
+        nc.sync.dma_start(idx4[:], offs4)
+
         identity = keep.tile([P, P], F32, name="identity")
         make_identity(nc, identity[:])
 
+        w1_codes = keep.tile([P, PASSES * 2 * H], U8, name="w1_codes", align_bytes=64)
+        nc.vector.tensor_copy(
+            w1_codes[:].bitcast(I32).rearrange("p (a t u w) -> p a t u w", a=PASSES, t=PACK, w=2),
+            w1_raw[:].bitcast(I32).rearrange("p (a u t w) -> p a t u w", a=PASSES, t=PACK, w=2),
+        )
         picked_sc = keep.tile([P, S], U8, name="picked_sc", tag="slot_picked", align_bytes=64)
         nc.vector.tensor_copy(picked_sc[:], tab_sc[:].indirect(idx[:]))
-        v_sc = keep.tile([P, PASSES, S], U8, name="v_sc", align_bytes=64)
+
+        page_rows = page0.rearrange("(u t e) c -> t u e c", t=PACK, e=RUN)
+        page_slots = ("slot0", "slot2", "slot3", "slot_picked")
+        page = [keep.tile([P, T2], F32, name="page0", tag=page_slots[0], align_bytes=64)]
+        nc.sync.dma_start(page[0][:], page_rows[0])
+
+        v_sc = [keep.tile([P, S], U8, name=f"v_sc{a}", align_bytes=64) for a in range(PASSES)]
         for a in range(PASSES):
             for h in range(2):
                 first = SPARE + 4 * (2 * a + h)
                 nc.sync.dma_start(
-                    v_sc[64 * h : 64 * h + 64, a, :].bitcast(I32), picked_sc[first : first + 64, :].bitcast(I32)
+                    v_sc[a][64 * h : 64 * h + 64, :].bitcast(I32), picked_sc[first : first + 64, :].bitcast(I32)
                 )
-
-        nc.sync.dma_start(tab[2][:], tab_rows[2])
         nc.sync.dma_start(idx2[:], offs2)
-        row_constants = keep.tile([P, 2, 8], F32, name="row_constants", align_bytes=64)
-        bias, gains = row_constants[:, 0, :], row_constants[:, 1, :]
-        nc.sync.dma_start(bias[:, :PACK], b1.rearrange("(p t) -> p t", t=PACK))
-        nc.sync.dma_start(gains[:, :PACK], gain.rearrange("(p t) -> p t", t=PACK))
 
-        w1_codes = keep.tile([P, PASSES * 2 * H], U8, name="w1_codes", tag="slot_codes", align_bytes=64)
-        nc.vector.tensor_copy(
-            w1_codes[:].bitcast(U16).rearrange("p (a t c i) -> p a c t i", a=PASSES, t=PACK, i=8),
-            w1_raw[:].bitcast(U16).rearrange("p (a c i t) -> p a c t i", a=PASSES, t=PACK, i=8),
-        )
         w1_sc = keep.tile([P, PASSES * H], U8, name="w1_sc", align_bytes=64)
         nc.vector.tensor_copy(
-            w1_sc[:].rearrange("p (a t c i) -> p a c t i", a=PASSES, t=PACK, i=16),
-            w1_sc_raw[:].rearrange("p (a c i t) -> p a c t i", a=PASSES, t=PACK, i=16),
+            w1_sc[:].bitcast(I32).rearrange("p (a t c i) -> p a c t i", a=PASSES, t=PACK, i=4),
+            w1_sc_raw[:].bitcast(I32).rearrange("p (a c i t) -> p a c t i", a=PASSES, t=PACK, i=4),
         )
 
         v = [[keep.tile([P, BANK], U32, name=f"v{a}_{h}", tag=f"slot_v{a}_{h}", align_bytes=64) for h in range(2)] for a in range(PASSES)]
@@ -110,39 +121,50 @@ def tile_list_rivet_growth_features_kernel(
             for h in range(2):
                 nc.vector.tensor_copy(v[a][h][:], tab[a][:].bitcast(U32).indirect(entries(idx, h * BANK, BANK)))
 
-        page_rows = page0.rearrange("(p t) c -> p t c", t=PACK)
-        page = [keep.tile([P, T2], F32, name=f"page{t}", tag=f"slot{t}", align_bytes=64) for t in range(PACK)]
-        nc.sync.dma_start(idx4[:], offs4)
-        nc.sync.dma_start(page[0][:], page_rows[:, 0, :])
+        wgs_raw.append(keep.tile([P, BANK], F32, name="wgs_raw1", tag="slot1", align_bytes=64))
+        nc.sync.dma_start(wgs_raw[1][:], wgs[:, BANK:])
         nc.sync.dma_start(idx3[:], offs3)
-        old_first = keep.tile([P, M], F32, name="old_first", align_bytes=64)
-        nc.vector.tensor_copy(old_first[:], page[0][:].indirect(idx4[:]))
         for t in range(1, PACK):
-            nc.sync.dma_start(page[t][:], page_rows[:, t, :])
+            page.append(keep.tile([P, T2], F32, name=f"page{t}", tag=page_slots[t], align_bytes=64))
+            nc.sync.dma_start(page[t][:], page_rows[t])
+
+        constant_dealt = keep.tile([P, PACK, P], F32, name="constant_dealt", align_bytes=64)
+        nc.scalar.copy(
+            constant_dealt[:].rearrange("p t (u e) -> p t u e", e=RUN),
+            constant_rows[:].rearrange("p (u t e) -> p t u e", t=PACK, e=RUN),
+        )
+        constant_bank = psum.tile([P, PACK, P], F32, name="y_bank", bufs=6)
+        for t in range(PACK):
+            nc.tensor.transpose(constant_bank[:, t, :], constant_dealt[:, t, :], identity[:])
+        gains = keep.tile([P, PACK], F32, name="gains", align_bytes=64)
+        nc.scalar.copy(gains[:], constant_bank[:, :, 31])
+        bias = []
+        for t in range(PACK):
+            bias.append(keep.tile([P, 1], F32, name=f"bias{t}", tag=f"slot_dealt{t + 1}", align_bytes=64))
+            nc.scalar.copy(bias[t][:], constant_bank[:, t, 30:31])
 
         turned = []
-        for h in range(2):
-            bank = psum.tile([P, PACK, P], F32, name="y_bank", bufs=6)
-            for i in range(PACK):
-                first = h * BANK + i * P
-                nc.tensor.transpose(bank[:, i, :], wgs_raw[:, first : first + P], identity[:])
-            turned.append(bank)
-
+        old_early = []
         for t in range(PACK):
+            if t < EARLY:
+                slot = "slot_old" if t == 0 else f"slot_weight{t - 1}"
+                old_early.append(keep.tile([P, M], F32, name=f"old_early{t}", tag=slot, align_bytes=64))
+                nc.vector.tensor_copy(old_early[t][:], page[t][:].indirect(idx4[:]))
             squashed = keep.tile([P, S], F32, name=f"squashed{t}")
             weight = keep.tile([P, S], F32, name=f"weight{t}", tag=f"slot_weight{t}", align_bytes=64)
-            for h in range(2):
-                dealt = ring.tile([P, PACK, 4, 32], F32, name="dealt", bufs=2)
-                rows = turned[h][:].rearrange("j i (u t) -> j t i u", t=PACK)[:, t]
-                nc.scalar.copy(dealt[:], rows.unsqueeze(2).to_broadcast([P, PACK, 4, 32]))
-                bank = psum.tile([P, PACK, P], F32, name="y_bank", bufs=6)
-                for i in range(PACK):
-                    nc.tensor.transpose(bank[:, i, :], dealt[:, i].rearrange("j q u -> j (q u)"), identity[:])
-                nc.scalar.activation(
-                    weight[:, h * BANK : (h + 1) * BANK], bank[:].rearrange("p i j -> p (i j)"), COPY, scale=gains[:, t : t + 1]
-                )
+            dealt = keep.tile([P, 2, PACK, 4, 8, RUN], F32, name=f"dealt{t}", tag=f"slot_dealt{t}", align_bytes=64)
             for h in range(2):
                 cols = slice(h * BANK, (h + 1) * BANK)
+                if t == 0:
+                    turned.append(psum.tile([P, PACK, P], F32, name="y_bank", bufs=6))
+                    for i in range(PACK):
+                        nc.tensor.transpose(turned[h][:, i, :], wgs_raw[h][:, i * P : (i + 1) * P], identity[:])
+                rows = turned[h][:].rearrange("j i (u t e) -> j t i u e", t=PACK, e=RUN)[:, t]
+                nc.scalar.copy(dealt[:, h], rows.unsqueeze(2).to_broadcast([P, PACK, 4, 8, RUN]))
+                bank = psum.tile([P, PACK, P], F32, name="y_bank", bufs=6)
+                for i in range(PACK):
+                    nc.tensor.transpose(bank[:, i, :], dealt[:, h, i].rearrange("j q u e -> j (q u e)"), identity[:])
+                nc.scalar.activation(weight[:, cols], bank[:].rearrange("p i j -> p (i j)"), COPY, scale=gains[:, t : t + 1])
                 acc = psum.tile([P, BANK], F32, name="h_bank", bufs=2)
                 for a in range(PASSES):
                     first = (a * PACK + t) * P
@@ -151,11 +173,11 @@ def tile_list_rivet_growth_features_kernel(
                         lhsT=w1_codes[:, 2 * first : 2 * (first + P)].bitcast(FP4X4),
                         lhsT_scale=w1_sc[:, first : first + P],
                         rhs=v[a][h][:].bitcast(FP8X4),
-                        rhs_scale=v_sc[:, a, cols],
+                        rhs_scale=v_sc[a][:, cols],
                         start=(a == 0),
                         stop=(a == PASSES - 1),
                     )
-                nc.scalar.activation(squashed[:, cols], acc[:], TANH, bias=bias[:, t : t + 1])
+                nc.scalar.activation(squashed[:, cols], acc[:], TANH, bias=bias[t][:])
             width = BANK if t == 0 else S
             for first in range(0, S, width):
                 cols = slice(first, first + width)
@@ -164,11 +186,12 @@ def tile_list_rivet_growth_features_kernel(
                 )
 
         w2_raw = keep.tile([P, PACK, N], F32, name="w2_raw", tag="slot_v0_0", align_bytes=64)
-        nc.sync.dma_start(w2_raw[:], w2.rearrange("(p j) n -> p j n", j=PACK))
+        for t in range(PACK):
+            nc.sync.dma_start(w2_raw[:, t, :], w2.rearrange("(u t e) n -> t u e n", t=PACK, e=RUN)[t])
         before = {}
-        for t in range(1, PACK):
+        for t in range(EARLY, PACK):
             before[t] = keep.tile([P, T2], F32, name=f"before{t}", tag=f"slot_v{t - 1}_1", align_bytes=64)
-            nc.sync.dma_start(before[t][:], page_rows[:, t, :])
+            nc.sync.dma_start(before[t][:], page_rows[t])
         w2_bf = keep.tile([P, GROUPS, PACK, P, PACK], BF16, name="w2_bf", align_bytes=64)
         for g in range(GROUPS):
             nc.scalar.copy(
@@ -177,9 +200,6 @@ def tile_list_rivet_growth_features_kernel(
             )
         w2_codes = keep.tile([P, N], U32, name="w2_codes", tag=f"slot_weight{PACK - 1}", align_bytes=64)
         w2_sc = keep.tile([P, N], U8, name="w2_sc", align_bytes=64)
-        nc.vector.quantize_mx(
-            out=w2_codes[:].bitcast(FP8X4), scales=w2_sc[:], in_=w2_bf[:].rearrange("p g t m j -> p (g t m j)")
-        )
 
         y_rows = out_0.rearrange("(g p t) m -> g p t m", g=GROUPS, t=PACK)
         y_words = out_1.rearrange("g p m t -> p g (m t)").bitcast(I32)
@@ -188,10 +208,9 @@ def tile_list_rivet_growth_features_kernel(
         last = len(WIDTHS) - 1
         old = {}
         banks = {}
-        codes = {}
 
         def fetch_old(k):
-            for t in range(1, PACK):
+            for t in range(EARLY, PACK):
                 old[k, t] = ring.tile([P, WIDTHS[k]], F32, name=f"old{t}", bufs=1, align_bytes=64)
                 nc.vector.tensor_copy(old[k, t][:], before[t][:].indirect(entries(idx4, starts[k], WIDTHS[k])))
 
@@ -199,11 +218,14 @@ def tile_list_rivet_growth_features_kernel(
             width = WIDTHS[k]
             x = ring.tile([P, PACK, width], F32, name="x", bufs=1)
             for t in range(PACK):
-                reference = old_first[:, starts[k] : starts[k] + width] if t == 0 else old[k, t][:]
+                reference = old_early[t][:, starts[k] : starts[k] + width] if t < EARLY else old[k, t][:]
                 nc.vector.tensor_tensor(x[:, t, :], page[t][:].indirect(entries(idx3, starts[k], width)), reference, SUBTRACT)
             x_bf = ring.tile([P, width, PACK], BF16, name="x_bf", bufs=2, align_bytes=64)
-            copy = nc.vector.tensor_copy if k == last else nc.scalar.copy
-            copy(x_bf[:].rearrange("p (c i) t -> p c t i", i=4), x[:].rearrange("p t (c i) -> p c t i", i=4))
+            if k == 0:
+                nc.vector.quantize_mx(
+                    out=w2_codes[:].bitcast(FP8X4), scales=w2_sc[:], in_=w2_bf[:].rearrange("p g t m j -> p (g t m j)")
+                )
+            nc.scalar.copy(x_bf[:].rearrange("p (c i) t -> p c t i", i=4), x[:].rearrange("p t (c i) -> p c t i", i=4))
             x_codes = ring.tile([P, width], U32, name="x_codes", bufs=2, align_bytes=64)
             x_sc = ring.tile([P, width], U8, name="x_sc", bufs=2, align_bytes=64)
             nc.vector.quantize_mx(out=x_codes[:].bitcast(FP8X4), scales=x_sc[:], in_=x_bf[:].rearrange("p m t -> p (m t)"))
@@ -226,20 +248,22 @@ def tile_list_rivet_growth_features_kernel(
         def hand_out(k, g):
             width = WIDTHS[k]
             cols = slice(starts[k], starts[k] + width)
-            if g == 0:
-                codes[k] = ring.tile([P, GROUPS, width], I32, name="y_codes", bufs=3, align_bytes=64)
-            copy = nc.vector.tensor_copy if (k, g) == (last, GROUPS - 1) else nc.scalar.copy
             y = ring.tile([P, PACK, width], F32, name="y", bufs=4)
             y_bf = ring.tile([P, width, PACK], BF16, name="y_bf", bufs=4, align_bytes=64)
+            y_codes = ring.tile([P, width], I32, name="y_codes", bufs=4, align_bytes=64)
             for first in range(0, width, UNIT):
-                copy(y_bf[:, first : first + UNIT, :], banks[k, g, first][:].rearrange("p t m -> p m t"))
-                copy(y[:, :, first : first + UNIT], banks[k, g, first][:])
+                nc.scalar.copy(y[:, :, first : first + UNIT], banks[k, g, first][:])
+                if k < SHARED_FROM:
+                    nc.scalar.copy(y_bf[:, first : first + UNIT, :], banks[k, g, first][:].rearrange("p t m -> p m t"))
             nc.sync.dma_start(y_rows[g][:, :, cols], y[:])
+            if k >= SHARED_FROM:
+                nc.vector.tensor_copy(
+                    y_bf[:].rearrange("p (c i) t -> p c t i", i=4), y[:].rearrange("p t (c i) -> p c t i", i=4)
+                )
             nc.vector.quantize_mx(
-                out=codes[k][:, g, :].bitcast(FP8X4), scales=y_sc[:, g, cols], in_=y_bf[:].rearrange("p m t -> p (m t)")
+                out=y_codes[:].bitcast(FP8X4), scales=y_sc[:, g, cols], in_=y_bf[:].rearrange("p m t -> p (m t)")
             )
-            if g == GROUPS - 1:
-                nc.sync.dma_start(y_words[:, :, cols], codes[k][:])
+            nc.sync.dma_start(y_words[:, g, cols], y_codes[:])
 
         fetch_old(0)
         for k in range(len(WIDTHS)):

from contextlib import ExitStack

import concourse.mybir as mybir
from concourse.masks import make_identity

K, T, S, H, T2, M, N = 1536, 2048, 1024, 512, 2048, 1024, 1024
FLOPS = 2 * K * H * S + 2 * H * N * M

F32 = mybir.dt.float32
BF16 = mybir.dt.bfloat16
I32 = mybir.dt.int32
U32 = mybir.dt.uint32
U16 = mybir.dt.uint16
U8 = mybir.dt.uint8
FP8X4 = mybir.dt.float8_e4m3fn_x4
FP4X4 = mybir.dt.float4_e2m1fn_x4
MULT = mybir.AluOpType.mult
SUBTRACT = mybir.AluOpType.subtract
TANH = mybir.ActivationFunctionType.Tanh
COPY = mybir.ActivationFunctionType.Copy

P = 128
PACK = 4
PASSES = K // (P * PACK)
GROUPS = N // (P * PACK)
BANK = 512
UNIT = 128
WIDTHS = (256, 256, 256, 256)
SPARE = 8
RUN = 4
EARLY = 2
SHARED_FROM = 2


def entries(offsets, first, count):
    return offsets[:, first // 16 : (first + count) // 16]


def tile_list_rivet_growth_features_kernel(
    tc, tab_words, tab_scales, offs, w1_words, w1_scales, b1, gain, page0, wgs, offs2, offs3, offs4, w2, out_0, out_1, out_2
):
    nc = tc.nc
    with ExitStack() as ctx:
        keep = ctx.enter_context(tc.tile_pool(name="keep", bufs=1))
        ring = ctx.enter_context(tc.tile_pool(name="ring", bufs=1))
        psum = ctx.enter_context(tc.psum_pool(name="psum", bufs=8))

        idx = keep.tile([P, S // 16], U16, name="idx")
        idx2 = keep.tile([P, S // 16], U16, name="idx2")
        idx3 = keep.tile([P, M // 16], U16, name="idx3")
        idx4 = keep.tile([P, M // 16], U16, name="idx4")
        w1_raw = keep.tile([P, PASSES * 2 * H], U8, name="w1_raw", align_bytes=64)
        nc.sync.dma_start(
            w1_raw[:].bitcast(I32).rearrange("p (a c) -> p a c", a=PASSES), w1_words.bitcast(I32).rearrange("a p c -> p a c")
        )
        nc.sync.dma_start(idx[:], offs)

        tab_sc = keep.tile([P, T], U8, name="tab_sc", tag="slot0", align_bytes=64)
        for rows in (slice(0, SPARE), slice(32, 32 + SPARE), slice(64, P)):
            nc.vector.memset(tab_sc[rows, :].bitcast(I32), 0)
        runs = tab_scales.rearrange("a (h e r) t -> e (a h) r t", e=2, r=4).bitcast(I32)
        for e in range(2):
            for first, count in ((0, 4), (4, 2)):
                rows = slice(32 * e + SPARE + 4 * first, 32 * e + SPARE + 4 * (first + count))
                nc.sync.dma_start(tab_sc[rows, :].bitcast(I32), runs[e, first : first + count])

        tab = [keep.tile([P, T], I32, name=f"tab{a}", tag=f"slot{a + 1}", align_bytes=64) for a in range(PASSES)]
        tab_rows = tab_words.rearrange("a p t i -> a p (t i)").bitcast(I32)
        for a in range(PASSES - 1):
            nc.sync.dma_start(tab[a][:], tab_rows[a])
        constant_rows = keep.tile([P, H], F32, name="constant_rows", align_bytes=64)
        for rows in (slice(0, 30), slice(32, 64), slice(64, P)):
            nc.gpsimd.memset(constant_rows[rows, :], 0.0)
        nc.sync.dma_start(constant_rows[30:31, :], b1.rearrange("(o r) -> o r", o=1))
        nc.sync.dma_start(constant_rows[31:32, :], gain.rearrange("(o r) -> o r", o=1))
        nc.sync.dma_start(tab[PASSES - 1][:], tab_rows[PASSES - 1])
        wgs_raw = [keep.tile([P, BANK], F32, name="wgs_raw0", align_bytes=64)]
        nc.sync.dma_start(wgs_raw[0][:], wgs[:, :BANK])
        w1_sc_raw = keep.tile([P, PASSES * H], U8, name="w1_sc_raw", align_bytes=64)
        nc.gpsimd.memset(w1_sc_raw[:].bitcast(I32), 0)
        for q in range(4):
            nc.sync.dma_start(
                w1_sc_raw[32 * q : 32 * q + 4, :].bitcast(I32).rearrange("r (a c) -> r a c", a=PASSES),
                w1_scales.bitcast(I32)[:, 4 * q : 4 * q + 4, :].rearrange("a r c -> r a c"),
            )
        nc.sync.dma_start(idx4[:], offs4)

        identity = keep.tile([P, P], F32, name="identity")
        make_identity(nc, identity[:])

        w1_codes = keep.tile([P, PASSES * 2 * H], U8, name="w1_codes", align_bytes=64)
        nc.vector.tensor_copy(
            w1_codes[:].bitcast(I32).rearrange("p (a t u w) -> p a t u w", a=PASSES, t=PACK, w=2),
            w1_raw[:].bitcast(I32).rearrange("p (a u t w) -> p a t u w", a=PASSES, t=PACK, w=2),
        )
        picked_sc = keep.tile([P, S], U8, name="picked_sc", tag="slot_picked", align_bytes=64)
        nc.vector.tensor_copy(picked_sc[:], tab_sc[:].indirect(idx[:]))

        page_rows = page0.rearrange("(u t e) c -> t u e c", t=PACK, e=RUN)
        page_slots = ("slot0", "slot2", "slot3", "slot_picked")
        page = [keep.tile([P, T2], F32, name="page0", tag=page_slots[0], align_bytes=64)]
        nc.sync.dma_start(page[0][:], page_rows[0])

        v_sc = [keep.tile([P, S], U8, name=f"v_sc{a}", align_bytes=64) for a in range(PASSES)]
        for a in range(PASSES):
            for h in range(2):
                first = SPARE + 4 * (2 * a + h)
                nc.sync.dma_start(
                    v_sc[a][64 * h : 64 * h + 64, :].bitcast(I32), picked_sc[first : first + 64, :].bitcast(I32)
                )
        nc.sync.dma_start(idx2[:], offs2)

        w1_sc = keep.tile([P, PASSES * H], U8, name="w1_sc", align_bytes=64)
        nc.vector.tensor_copy(
            w1_sc[:].bitcast(I32).rearrange("p (a t c i) -> p a c t i", a=PASSES, t=PACK, i=4),
            w1_sc_raw[:].bitcast(I32).rearrange("p (a c i t) -> p a c t i", a=PASSES, t=PACK, i=4),
        )

        v = [[keep.tile([P, BANK], U32, name=f"v{a}_{h}", tag=f"slot_v{a}_{h}", align_bytes=64) for h in range(2)] for a in range(PASSES)]
        for a in range(PASSES):
            for h in range(2):
                nc.vector.tensor_copy(v[a][h][:], tab[a][:].bitcast(U32).indirect(entries(idx, h * BANK, BANK)))

        wgs_raw.append(keep.tile([P, BANK], F32, name="wgs_raw1", tag="slot1", align_bytes=64))
        nc.sync.dma_start(wgs_raw[1][:], wgs[:, BANK:])
        nc.sync.dma_start(idx3[:], offs3)
        for t in range(1, PACK):
            page.append(keep.tile([P, T2], F32, name=f"page{t}", tag=page_slots[t], align_bytes=64))
            nc.sync.dma_start(page[t][:], page_rows[t])

        constant_dealt = keep.tile([P, PACK, P], F32, name="constant_dealt", align_bytes=64)
        nc.scalar.copy(
            constant_dealt[:].rearrange("p t (u e) -> p t u e", e=RUN),
            constant_rows[:].rearrange("p (u t e) -> p t u e", t=PACK, e=RUN),
        )
        constant_bank = psum.tile([P, PACK, P], F32, name="y_bank", bufs=6)
        for t in range(PACK):
            nc.tensor.transpose(constant_bank[:, t, :], constant_dealt[:, t, :], identity[:])
        gains = keep.tile([P, PACK], F32, name="gains", align_bytes=64)
        nc.scalar.copy(gains[:], constant_bank[:, :, 31])
        bias = []
        for t in range(PACK):
            bias.append(keep.tile([P, 1], F32, name=f"bias{t}", tag=f"slot_dealt{t + 1}", align_bytes=64))
            nc.scalar.copy(bias[t][:], constant_bank[:, t, 30:31])

        turned = []
        old_early = []
        for t in range(PACK):
            if t < EARLY:
                slot = "slot_old" if t == 0 else f"slot_weight{t - 1}"
                old_early.append(keep.tile([P, M], F32, name=f"old_early{t}", tag=slot, align_bytes=64))
                nc.vector.tensor_copy(old_early[t][:], page[t][:].indirect(idx4[:]))
            squashed = keep.tile([P, S], F32, name=f"squashed{t}")
            weight = keep.tile([P, S], F32, name=f"weight{t}", tag=f"slot_weight{t}", align_bytes=64)
            dealt = keep.tile([P, 2, PACK, 4, 8, RUN], F32, name=f"dealt{t}", tag=f"slot_dealt{t}", align_bytes=64)
            for h in range(2):
                cols = slice(h * BANK, (h + 1) * BANK)
                if t == 0:
                    turned.append(psum.tile([P, PACK, P], F32, name="y_bank", bufs=6))
                    for i in range(PACK):
                        nc.tensor.transpose(turned[h][:, i, :], wgs_raw[h][:, i * P : (i + 1) * P], identity[:])
                rows = turned[h][:].rearrange("j i (u t e) -> j t i u e", t=PACK, e=RUN)[:, t]
                nc.scalar.copy(dealt[:, h], rows.unsqueeze(2).to_broadcast([P, PACK, 4, 8, RUN]))
                bank = psum.tile([P, PACK, P], F32, name="y_bank", bufs=6)
                for i in range(PACK):
                    nc.tensor.transpose(bank[:, i, :], dealt[:, h, i].rearrange("j q u e -> j (q u e)"), identity[:])
                nc.scalar.activation(weight[:, cols], bank[:].rearrange("p i j -> p (i j)"), COPY, scale=gains[:, t : t + 1])
                acc = psum.tile([P, BANK], F32, name="h_bank", bufs=2)
                for a in range(PASSES):
                    first = (a * PACK + t) * P
                    nc.tensor.matmul_mx(
                        out=acc[:],
                        lhsT=w1_codes[:, 2 * first : 2 * (first + P)].bitcast(FP4X4),
                        lhsT_scale=w1_sc[:, first : first + P],
                        rhs=v[a][h][:].bitcast(FP8X4),
                        rhs_scale=v_sc[a][:, cols],
                        start=(a == 0),
                        stop=(a == PASSES - 1),
                    )
                nc.scalar.activation(squashed[:, cols], acc[:], TANH, bias=bias[t][:])
            width = BANK if t == 0 else S
            for first in range(0, S, width):
                cols = slice(first, first + width)
                nc.vector.tensor_tensor(
                    page[t][:].indirect(entries(idx2, first, width)), squashed[:, cols], weight[:, cols], MULT
                )

        w2_raw = keep.tile([P, PACK, N], F32, name="w2_raw", tag="slot_v0_0", align_bytes=64)
        for t in range(PACK):
            nc.sync.dma_start(w2_raw[:, t, :], w2.rearrange("(u t e) n -> t u e n", t=PACK, e=RUN)[t])
        before = {}
        for t in range(EARLY, PACK):
            before[t] = keep.tile([P, T2], F32, name=f"before{t}", tag=f"slot_v{t - 1}_1", align_bytes=64)
            nc.sync.dma_start(before[t][:], page_rows[t])
        w2_bf = keep.tile([P, GROUPS, PACK, P, PACK], BF16, name="w2_bf", align_bytes=64)
        for g in range(GROUPS):
            nc.scalar.copy(
                w2_bf[:, g].rearrange("p t m j -> p m t j"),
                w2_raw[:, :, g * BANK : (g + 1) * BANK].rearrange("p j (m t) -> p m t j", t=PACK),
            )
        w2_codes = keep.tile([P, N], U32, name="w2_codes", tag=f"slot_weight{PACK - 1}", align_bytes=64)
        w2_sc = keep.tile([P, N], U8, name="w2_sc", align_bytes=64)

        y_rows = out_0.rearrange("(g p t) m -> g p t m", g=GROUPS, t=PACK)
        y_words = out_1.rearrange("g p m t -> p g (m t)").bitcast(I32)
        y_sc = keep.tile([P, GROUPS, M], U8, name="y_sc", align_bytes=64)
        starts = [sum(WIDTHS[:k]) for k in range(len(WIDTHS))]
        last = len(WIDTHS) - 1
        old = {}
        banks = {}

        def fetch_old(k):
            for t in range(EARLY, PACK):
                old[k, t] = ring.tile([P, WIDTHS[k]], F32, name=f"old{t}", bufs=1, align_bytes=64)
                nc.vector.tensor_copy(old[k, t][:], before[t][:].indirect(entries(idx4, starts[k], WIDTHS[k])))

        def multiply(k):
            width = WIDTHS[k]
            x = ring.tile([P, PACK, width], F32, name="x", bufs=1)
            for t in range(PACK):
                reference = old_early[t][:, starts[k] : starts[k] + width] if t < EARLY else old[k, t][:]
                nc.vector.tensor_tensor(x[:, t, :], page[t][:].indirect(entries(idx3, starts[k], width)), reference, SUBTRACT)
            x_bf = ring.tile([P, width, PACK], BF16, name="x_bf", bufs=2, align_bytes=64)
            if k == 0:
                nc.vector.quantize_mx(
                    out=w2_codes[:].bitcast(FP8X4), scales=w2_sc[:], in_=w2_bf[:].rearrange("p g t m j -> p (g t m j)")
                )
            nc.scalar.copy(x_bf[:].rearrange("p (c i) t -> p c t i", i=4), x[:].rearrange("p t (c i) -> p c t i", i=4))
            x_codes = ring.tile([P, width], U32, name="x_codes", bufs=2, align_bytes=64)
            x_sc = ring.tile([P, width], U8, name="x_sc", bufs=2, align_bytes=64)
            nc.vector.quantize_mx(out=x_codes[:].bitcast(FP8X4), scales=x_sc[:], in_=x_bf[:].rearrange("p m t -> p (m t)"))
            for g in range(GROUPS):
                for first in range(0, width, UNIT):
                    acc = psum.tile([P, PACK, UNIT], F32, name="y_bank", bufs=6)
                    for t in range(PACK):
                        stationary = slice((g * PACK + t) * P, (g * PACK + t + 1) * P)
                        nc.tensor.matmul_mx(
                            out=acc[:, t, :],
                            lhsT=w2_codes[:, stationary].bitcast(FP8X4),
                            lhsT_scale=w2_sc[:, stationary],
                            rhs=x_codes[:, first : first + UNIT].bitcast(FP8X4),
                            rhs_scale=x_sc[:, first : first + UNIT],
                            start=True,
                            stop=True,
                        )
                    banks[k, g, first] = acc

        def hand_out(k, g):
            width = WIDTHS[k]
            cols = slice(starts[k], starts[k] + width)
            y = ring.tile([P, PACK, width], F32, name="y", bufs=4)
            y_bf = ring.tile([P, width, PACK], BF16, name="y_bf", bufs=4, align_bytes=64)
            y_codes = ring.tile([P, width], I32, name="y_codes", bufs=4, align_bytes=64)
            for first in range(0, width, UNIT):
                nc.scalar.copy(y[:, :, first : first + UNIT], banks[k, g, first][:])
                if k < SHARED_FROM:
                    nc.scalar.copy(y_bf[:, first : first + UNIT, :], banks[k, g, first][:].rearrange("p t m -> p m t"))
            nc.sync.dma_start(y_rows[g][:, :, cols], y[:])
            if k >= SHARED_FROM:
                nc.vector.tensor_copy(
                    y_bf[:].rearrange("p (c i) t -> p c t i", i=4), y[:].rearrange("p t (c i) -> p c t i", i=4)
                )
            nc.vector.quantize_mx(
                out=y_codes[:].bitcast(FP8X4), scales=y_sc[:, g, cols], in_=y_bf[:].rearrange("p m t -> p (m t)")
            )
            nc.sync.dma_start(y_words[:, g, cols], y_codes[:])

        fetch_old(0)
        for k in range(len(WIDTHS)):
            multiply(k)
            if k < last:
                fetch_old(k + 1)
            if k > 0:
                hand_out(k - 1, 1)
            hand_out(k, 0)
        hand_out(last, 1)
        for q in range(4):
            nc.sync.dma_start(
                out_2.bitcast(I32)[:, 4 * q : 4 * q + 4, :].rearrange("g r m -> r g m"), y_sc[32 * q : 32 * q + 4].bitcast(I32)
            )
